import numpy as np
import ml_dtypes


def mxq(x, axis, fmt="e4m3"):
    dtype, down = {"e4m3": (ml_dtypes.float8_e4m3fn, 7), "e5m2": (ml_dtypes.float8_e5m2, 14)}[fmt]
    v = np.moveaxis(np.asarray(x, np.float32).astype(ml_dtypes.bfloat16).astype(np.float64), axis, -1)
    blocks = v.reshape(v.shape[:-1] + (-1, 32))
    amax = np.abs(blocks).max(-1, keepdims=True)
    byte = np.maximum(np.where(amax > 0, np.frexp(amax)[1] - 1 + 127, 0) - down, 1)
    scale = np.exp2(byte - 127.0)
    codes = (blocks / scale).astype(np.float32).astype(dtype).astype(np.float64)
    return np.moveaxis((codes * scale).reshape(v.shape), -1, axis)


WIDE = False


def mx_kscale(k):
    if not WIDE:
        return np.ones(k)
    levels = np.array([10, -10, 5, -5, 0])
    if k % 512:
        return np.exp2(np.random.permutation(np.resize(levels, k // 32))).repeat(32)
    a = np.empty((k // 512, 16))
    for p in range(k // 512):
        a[p, :8] = np.random.permutation(np.resize(levels, 8))
        for g in range(8):
            far = levels[np.abs(levels - a[p, g]) >= 10]
            a[p, g + 8] = far[np.random.randint(len(far))]
    return np.exp2(a.ravel()).repeat(32)


BF16 = ml_dtypes.bfloat16


def bf(x):
    return np.asarray(x, np.float32).astype(BF16)


def f64(x):
    return np.asarray(x).astype(np.float64)


E2M1 = np.array([0.0, 0.5, 1.0, 1.5, 2.0, 3.0, 4.0, 6.0, -0.0, -0.5, -1.0, -1.5, -2.0, -3.0, -4.0, -6.0])


def pack_weight(w, fmt):
    k, n = w.shape
    w = f64(bf(w)).reshape(k // 32, 32, n)
    amax = np.abs(w).max(1)
    if fmt == "e4m3":
        byte = np.frexp(amax)[1] - 1 + 127 - 7
    else:
        mant, ex = np.frexp(amax / 6.0)
        byte = np.where(mant > 0.5, ex, ex - 1) + 127
    byte = np.clip(np.where(amax > 0, byte, 1), 1, 254)
    scaled = (w * np.exp2(127.0 - byte)[:, None, :]).reshape(k, n).astype(np.float32)
    by_word = np.ascontiguousarray(scaled.reshape(k // 512, 128, 4, n).transpose(0, 1, 3, 2))
    if fmt == "e4m3":
        words = by_word.astype(ml_dtypes.float8_e4m3fn).view(np.uint8)
    else:
        c = by_word.astype(ml_dtypes.float4_e2m1fn).view(np.uint8) & 0xF
        words = c[..., 0::2] | (c[..., 1::2] << 4)
    return np.ascontiguousarray(words), np.ascontiguousarray(byte.astype(np.uint8).reshape(k // 512, 16, n))


def unpack_weight(words, scales, fmt):
    g, p, n, _ = words.shape
    if fmt == "e4m3":
        vals = np.ascontiguousarray(words).view(ml_dtypes.float8_e4m3fn).astype(np.float64)
    else:
        nib = np.empty((g, p, n, 4), np.uint8)
        nib[..., 0::2] = words & 0xF
        nib[..., 1::2] = words >> 4
        vals = E2M1[nib]
    vals = vals * np.repeat(np.exp2(scales.astype(np.float64) - 127.0), 8, axis=1)[..., None]
    return vals.transpose(0, 1, 3, 2).reshape(g * 512, n)
def pack4(w):
    words, scales = pack_weight(w, "e2m1")
    return words.reshape(words.shape[0], 128, -1), scales


def unpack4(words, scales):
    return unpack_weight(words.reshape(words.shape[0], 128, -1, 2), scales, "e2m1")


H, T, D, L, R = 4, 1024, 512, 1024, 512


def setup_inputs():
    s = mx_kscale(H * D).reshape(H, D)
    t = mx_kscale(H * L).reshape(H, L)
    query = np.random.standard_normal((H, T, D)) * s[:, None, :]
    keys = np.random.standard_normal((H, D, L)) / np.sqrt(D) / s[:, :, None]
    sigma = L * np.random.uniform(0.4, 0.8, (H, T, 1))
    dist = np.abs(np.arange(T)[:, None] - np.arange(L))
    energy = 0.5 * np.square(dist / sigma)
    gain = 1 + 0.1 * np.random.standard_normal((H, 1, L))
    prior = np.exp(-energy) * gain * t[:, None, :]
    readout = np.random.standard_normal((H, L, R)) / np.sqrt(L) / t[:, :, None]
    key_words, key_scales = pack4(keys.reshape(H * D, L))
    read_words, read_scales = pack4(readout.reshape(H * L, R))
    return {"query": bf(query), "energy": bf(energy), "prior": bf(prior),
            "key_words": key_words, "key_scales": key_scales,
            "read_words": read_words, "read_scales": read_scales}


def reference(query, energy, prior, key_words, key_scales, read_words, read_scales):
    keys = unpack4(key_words, key_scales).reshape(H, D, L)
    readout = unpack4(read_words, read_scales).reshape(H, L, R)
    score = mxq(f64(query), 2, "e4m3") @ keys
    ratio = score + f64(energy)
    disc = np.square(ratio) * f64(prior)
    return mxq(disc, 2, "e4m3") @ readout

@@ -1,0 +1,276 @@
+from contextlib import ExitStack
+
+import concourse.mybir as mybir
+from concourse.masks import make_identity
+
+H, T, D, L, R = 4, 1024, 512, 1024, 512
+FLOPS = 2 * H * T * D * L + 2 * H * T * L * R
+
+F32 = mybir.dt.float32
+BF16 = mybir.dt.bfloat16
+I32 = mybir.dt.int32
+U32 = mybir.dt.uint32
+U8 = mybir.dt.uint8
+FP8X4 = mybir.dt.float8_e4m3fn_x4
+FP4X4 = mybir.dt.float4_e2m1fn_x4
+MULT = mybir.AluOpType.mult
+ADD = mybir.AluOpType.add
+SQUARE = mybir.ActivationFunctionType.Square
+
+P = 128
+TILES = T // P
+N_TILES = H * TILES
+N_PAIRS = N_TILES // 2
+LOOKAHEAD = 7
+
+
+def tile_anomaly_association_discrepancy_s14_kernel(
+    tc, query, energy, prior, key_words, key_scales, read_words, read_scales, out
+):
+    nc = tc.nc
+    q_view = query.rearrange("h (p j) d -> h p j d", j=TILES)
+    e_view = energy.rearrange("h (p j) l -> h p j l", j=TILES)
+    p_view = prior.rearrange("h (p j) l -> h p j l", j=TILES)
+    o_view = out.rearrange("h (p j) r -> h p j r", j=TILES)
+
+    with ExitStack() as ctx:
+        keep = ctx.enter_context(tc.tile_pool(name="keep", bufs=1))
+        load = ctx.enter_context(tc.tile_pool(name="load", bufs=LOOKAHEAD + 1))
+        work = ctx.enter_context(tc.tile_pool(name="work", bufs=3))
+        score_pool = ctx.enter_context(tc.psum_pool(name="score_pool", bufs=4))
+        turn_pool = ctx.enter_context(tc.psum_pool(name="turn_pool", bufs=2))
+        out_pool = ctx.enter_context(tc.psum_pool(name="out_pool", bufs=2))
+
+        ident = keep.tile([P, P], F32)
+        warm = keep.tile([P, 1], F32)
+        k_words = [keep.tile([P, 2 * L], U8, align_bytes=64, name="k_words%d" % h) for h in range(H)]
+        r_words = [keep.tile([P, 2, 2 * R], U8, align_bytes=64, name="r_words%d" % h) for h in range(H)]
+        k_scales = keep.tile([P, H, L], U8, align_bytes=64)
+        r_scales = keep.tile([P, 2 * H, R], U8, align_bytes=64)
+
+        q_tiles, e_tiles, p_tiles = {}, {}, {}
+        q_codes, q_planes, q_banks, q_groups = {}, {}, {}, {}
+        scores, ratios, squares, discs = {}, {}, {}, {}
+        d_banks, d_groups, d_codes, d_planes = {}, {}, {}, {}
+        o_banks, o_tiles = {}, {}
+
+        def where(m):
+            return m // (TILES // 2), slice(2 * (m % (TILES // 2)), 2 * (m % (TILES // 2)) + 2)
+
+        def load_query(m):
+            if m >= N_PAIRS:
+                return
+            h, js = where(m)
+            q_tiles[m] = load.tile([P, 2, D], BF16, name="q_tile")
+            nc.sync.dma_start(out=q_tiles[m][:], in_=q_view[h, :, js, :])
+
+        def load_energy(m):
+            h, js = where(m)
+            e_tiles[m] = load.tile([P, 2, L], BF16, name="e_tile")
+            nc.sync.dma_start(out=e_tiles[m][:], in_=e_view[h, :, js, :])
+
+        def load_prior(m):
+            h, js = where(m)
+            p_tiles[m] = load.tile([P, 2, L], BF16, name="p_tile")
+            nc.sync.dma_start(out=p_tiles[m][:], in_=p_view[h, :, js, :])
+
+        def load_keys(h):
+            nc.sync.dma_start(out=k_words[h][:].bitcast(I32), in_=key_words[h].bitcast(I32))
+
+        def load_readout(h):
+            nc.sync.dma_start(
+                out=r_words[h][:].bitcast(I32),
+                in_=read_words[2 * h : 2 * h + 2].bitcast(I32).rearrange("g p n -> p g n"),
+            )
+
+        def load_scales(plane, scales):
+            rows = scales.bitcast(I32).rearrange("g (q r) n -> r q g n", r=4)
+            for r in range(4):
+                nc.sync.dma_start(out=plane[r:P:32, :, :].bitcast(I32), in_=rows[r])
+
+        def load_pair(m):
+            if m >= N_PAIRS:
+                return
+            load_energy(m)
+            load_prior(m)
+            load_query(m + 2)
+            h, rest = divmod(m + 3, TILES // 2)
+            if rest == 0 and h < H:
+                load_keys(h)
+                load_readout(h)
+
+        def turn_query(m):
+            if m >= N_PAIRS:
+                return
+            bank = turn_pool.tile([P, 2, 2, P], F32, name="turn")
+            for j in range(2):
+                words = q_tiles[m][:, j, :].bitcast(F32)
+                for u in range(2):
+                    nc.tensor.transpose(bank[:, j, u, :], words[:, u : D // 2 : 2], ident[:])
+            q_banks[m] = bank
+            q_groups[m] = work.tile([P, 2 * P * 4], BF16, align_bytes=64, name="q_group", bufs=2)
+
+        def copy_query(m, j, copy):
+            if m >= N_PAIRS:
+                return
+            dst = q_groups[m][:].bitcast(F32).rearrange("p (j r u) -> p j r u", j=2, u=2)
+            copy(out=dst[:, j], in_=q_banks[m][:, j].rearrange("p u r -> p r u"))
+
+        def quantise_query(m):
+            if m >= N_PAIRS:
+                return
+            q_codes[m] = work.tile([P, 2 * P], U32, align_bytes=64, name="q_code")
+            q_planes[m] = work.tile([P, 2 * P], U8, align_bytes=64, name="q_plane")
+            nc.vector.quantize_mx(out=q_codes[m][:].bitcast(FP8X4), scales=q_planes[m][:], in_=q_groups[m][:])
+
+        def multiply_keys(n):
+            if n >= N_TILES:
+                return
+            m, h = n // 2, n // TILES
+            cols = slice((n % 2) * P, (n % 2) * P + P)
+            scores[n] = []
+            for half in range(2):
+                bank = score_pool.tile([P, 512], F32, name="score")
+                nc.tensor.matmul_mx(
+                    out=bank[:],
+                    lhsT=q_codes[m][:, cols].bitcast(FP8X4),
+                    lhsT_scale=q_planes[m][:, cols],
+                    rhs=k_words[h][:, 1024 * half : 1024 * half + 1024].bitcast(FP4X4),
+                    rhs_scale=k_scales[:, h, 512 * half : 512 * half + 512],
+                    start=True,
+                    stop=True,
+                )
+                scores[n].append(bank)
+
+        def add_energy(n):
+            if n >= N_TILES:
+                return
+            ratios[n] = work.tile([P, L], F32, name="ratio")
+            for half in range(2):
+                cols = slice(512 * half, 512 * half + 512)
+                nc.vector.tensor_tensor(
+                    out=ratios[n][:, cols], in0=scores[n][half][:], in1=e_tiles[n // 2][:, n % 2, cols], op=ADD
+                )
+
+        def square(n):
+            if n >= N_TILES:
+                return
+            squares[n] = work.tile([P, L], F32, name="square_tile")
+            nc.scalar.activation(out=squares[n][:], in_=ratios[n][:], func=SQUARE)
+            discs[n] = work.tile([P, L], BF16, align_bytes=64, name="disc")
+
+        def times_prior(n, half, engine):
+            if not 0 <= n < N_TILES:
+                return
+            cols = slice(512 * half, 512 * half + 512)
+            engine.tensor_tensor(
+                out=discs[n][:, cols].rearrange("p (u w e) -> p u w e", u=2, e=2),
+                in0=squares[n][:, cols].rearrange("p (w u e) -> p u w e", u=2, e=2),
+                in1=p_tiles[n // 2][:, n % 2, cols].rearrange("p (w u e) -> p u w e", u=2, e=2),
+                op=MULT,
+            )
+
+        def turn_disc(n):
+            if not 0 <= n < N_TILES:
+                return
+            bank = turn_pool.tile([P, 2, 2, P], F32, name="turn")
+            words = discs[n][:].bitcast(F32)
+            for s in range(4):
+                nc.tensor.transpose(bank[:, s // 2, s % 2, :], words[:, P * s : P * s + P], ident[:])
+            d_banks[n] = bank
+
+        def copy_disc(n):
+            if not 0 <= n < N_TILES:
+                return
+            d_groups[n] = work.tile([P, L], BF16, align_bytes=64, name="d_group")
+            nc.scalar.copy(
+                out=d_groups[n][:].bitcast(F32).rearrange("p (g r u) -> p g r u", g=2, u=2),
+                in_=d_banks[n][:].rearrange("p g u r -> p g r u"),
+            )
+
+        def quantise_disc(n):
+            if not 0 <= n < N_TILES:
+                return
+            d_codes[n] = work.tile([P, 2 * P], U32, align_bytes=64, name="d_code")
+            d_planes[n] = work.tile([P, 2 * P], U8, align_bytes=64, name="d_plane")
+            nc.vector.quantize_mx(out=d_codes[n][:].bitcast(FP8X4), scales=d_planes[n][:], in_=d_groups[n][:])
+
+        def multiply_readout(n):
+            if not 0 <= n < N_TILES:
+                return
+            h = n // TILES
+            o_banks[n] = out_pool.tile([P, R], F32, name="o_bank")
+            for g in range(2):
+                cols = slice(P * g, P * g + P)
+                nc.tensor.matmul_mx(
+                    out=o_banks[n][:],
+                    lhsT=d_codes[n][:, cols].bitcast(FP8X4),
+                    lhsT_scale=d_planes[n][:, cols],
+                    rhs=r_words[h][:, g, :].bitcast(FP4X4),
+                    rhs_scale=r_scales[:, 2 * h + g, :],
+                    start=(g == 0),
+                    stop=(g == 1),
+                )
+
+        def copy_out(n):
+            if not 0 <= n < N_TILES:
+                return
+            if n % 2 == 0:
+                o_tiles[n // 2] = work.tile([P, 2, R], F32, name="o_tile")
+            nc.scalar.copy(out=o_tiles[n // 2][:, n % 2, :], in_=o_banks[n][:])
+
+        def store(m):
+            h, js = where(m)
+            nc.sync.dma_start(out=o_view[h, :, js, :], in_=o_tiles[m][:])
+
+        make_identity(nc, ident[:])
+        nc.vector.memset(warm[:], 0.0)
+        nc.vector.memset(k_scales[:].bitcast(I32), 0)
+        nc.vector.memset(r_scales[:].bitcast(I32), 0)
+
+        with tc.manual_schedule():
+            nc.scalar.activation(out=warm[:], in_=warm[:], func=SQUARE)
+            load_query(0)
+            load_scales(k_scales, key_scales)
+            load_keys(0)
+            load_energy(0)
+            load_query(1)
+            load_prior(0)
+            load_query(2)
+            load_scales(r_scales, read_scales)
+            load_readout(0)
+            for m in range(1, LOOKAHEAD):
+                load_pair(m)
+
+            turn_query(0)
+            turn_query(1)
+            for m in range(2):
+                copy_query(m, 0, nc.vector.tensor_copy)
+                copy_query(m, 1, nc.scalar.copy)
+                if m == 0:
+                    quantise_query(m)
+            multiply_keys(0)
+            multiply_keys(1)
+
+            for n in range(N_TILES + 3):
+                add_energy(n)
+                copy_disc(n - 2)
+                copy_out(n - 3)
+                square(n)
+                times_prior(n - 1, 0, nc.vector)
+                times_prior(n, 1, nc.gpsimd)
+                quantise_disc(n - 2)
+                if n % 2:
+                    copy_query((n + 3) // 2, 0, nc.vector.tensor_copy)
+                    copy_query((n + 3) // 2, 1, nc.scalar.copy)
+                else:
+                    quantise_query((n + 2) // 2)
+                turn_disc(n - 1)
+                if n % 2 == 0:
+                    turn_query((n + 4) // 2)
+                multiply_readout(n - 2)
+                multiply_keys(n + 2)
+                if n % 2:
+                    load_pair((n - 1) // 2 + LOOKAHEAD)
+                elif n >= 4:
+                    store((n - 4) // 2)

@@ -255,7 +255,6 @@ def tile_anomaly_association_discrepancy_s14_kernel(
             for n in range(N_TILES + 3):
                 add_energy(n)
                 copy_disc(n - 2)
-                copy_out(n - 3)
                 square(n)
                 times_prior(n - 1, 0, nc.vector)
                 times_prior(n, 1, nc.gpsimd)
@@ -265,11 +264,12 @@ def tile_anomaly_association_discrepancy_s14_kernel(
                     copy_query((n + 3) // 2, 1, nc.scalar.copy)
                 else:
                     quantise_query((n + 2) // 2)
+                copy_out(n - 3)
                 turn_disc(n - 1)
                 if n % 2 == 0:
                     turn_query((n + 4) // 2)
-                multiply_readout(n - 2)
                 multiply_keys(n + 2)
+                multiply_readout(n - 2)
                 if n % 2:
                     load_pair((n - 1) // 2 + LOOKAHEAD)
                 elif n >= 4:

@@ -21,7 +21,7 @@ P = 128
 TILES = T // P
 N_TILES = H * TILES
 N_PAIRS = N_TILES // 2
-LOOKAHEAD = 7
+LOOKAHEAD = 5
 
 
 def tile_anomaly_association_discrepancy_s14_kernel(
@@ -56,6 +56,9 @@ def tile_anomaly_association_discrepancy_s14_kernel(
 
         def where(m):
             return m // (TILES // 2), slice(2 * (m % (TILES // 2)), 2 * (m % (TILES // 2)) + 2)
+
+        def parts(n):
+            return 2 if n == N_TILES - 1 else 1
 
         def load_query(m):
             if m >= N_PAIRS:
@@ -109,6 +112,8 @@ def tile_anomaly_association_discrepancy_s14_kernel(
                     nc.tensor.transpose(bank[:, j, u, :], words[:, u : D // 2 : 2], ident[:])
             q_banks[m] = bank
             q_groups[m] = work.tile([P, 2 * P * 4], BF16, align_bytes=64, name="q_group", bufs=2)
+            q_codes[m] = work.tile([P, 2 * P], U32, align_bytes=64, name="q_code")
+            q_planes[m] = work.tile([P, 2 * P], U8, align_bytes=64, name="q_plane")
 
         def copy_query(m, j, copy):
             if m >= N_PAIRS:
@@ -116,12 +121,15 @@ def tile_anomaly_association_discrepancy_s14_kernel(
             dst = q_groups[m][:].bitcast(F32).rearrange("p (j r u) -> p j r u", j=2, u=2)
             copy(out=dst[:, j], in_=q_banks[m][:, j].rearrange("p u r -> p r u"))
 
-        def quantise_query(m):
+        def quantise_query(m, j0, j1):
             if m >= N_PAIRS:
                 return
-            q_codes[m] = work.tile([P, 2 * P], U32, align_bytes=64, name="q_code")
-            q_planes[m] = work.tile([P, 2 * P], U8, align_bytes=64, name="q_plane")
-            nc.vector.quantize_mx(out=q_codes[m][:].bitcast(FP8X4), scales=q_planes[m][:], in_=q_groups[m][:])
+            cols = slice(P * j0, P * j1)
+            nc.vector.quantize_mx(
+                out=q_codes[m][:, cols].bitcast(FP8X4),
+                scales=q_planes[m][:, cols],
+                in_=q_groups[m][:, 4 * P * j0 : 4 * P * j1],
+            )
 
         def multiply_keys(n):
             if n >= N_TILES:
@@ -156,7 +164,9 @@ def tile_anomaly_association_discrepancy_s14_kernel(
             if n >= N_TILES:
                 return
             squares[n] = work.tile([P, L], F32, name="square_tile")
-            nc.scalar.activation(out=squares[n][:], in_=ratios[n][:], func=SQUARE)
+            width = L // parts(n)
+            for c in range(0, L, width):
+                nc.scalar.activation(out=squares[n][:, c : c + width], in_=ratios[n][:, c : c + width], func=SQUARE)
             discs[n] = work.tile([P, L], BF16, align_bytes=64, name="disc")
 
         def times_prior(n, half, engine):
@@ -183,17 +193,24 @@ def tile_anomaly_association_discrepancy_s14_kernel(
             if not 0 <= n < N_TILES:
                 return
             d_groups[n] = work.tile([P, L], BF16, align_bytes=64, name="d_group")
-            nc.scalar.copy(
-                out=d_groups[n][:].bitcast(F32).rearrange("p (g r u) -> p g r u", g=2, u=2),
-                in_=d_banks[n][:].rearrange("p g u r -> p g r u"),
-            )
+            dst = d_groups[n][:].bitcast(F32).rearrange("p (g r u) -> p g r u", g=2, u=2)
+            src = d_banks[n][:].rearrange("p g u r -> p g r u")
+            width = 2 // parts(n)
+            for g in range(0, 2, width):
+                nc.scalar.copy(out=dst[:, g : g + width], in_=src[:, g : g + width])
 
         def quantise_disc(n):
             if not 0 <= n < N_TILES:
                 return
             d_codes[n] = work.tile([P, 2 * P], U32, align_bytes=64, name="d_code")
             d_planes[n] = work.tile([P, 2 * P], U8, align_bytes=64, name="d_plane")
-            nc.vector.quantize_mx(out=d_codes[n][:].bitcast(FP8X4), scales=d_planes[n][:], in_=d_groups[n][:])
+            width = 2 * P // parts(n)
+            for c in range(0, 2 * P, width):
+                nc.vector.quantize_mx(
+                    out=d_codes[n][:, c : c + width].bitcast(FP8X4),
+                    scales=d_planes[n][:, c : c + width],
+                    in_=d_groups[n][:, 4 * c : 4 * (c + width)],
+                )
 
         def multiply_readout(n):
             if not 0 <= n < N_TILES:
@@ -216,12 +233,12 @@ def tile_anomaly_association_discrepancy_s14_kernel(
             if not 0 <= n < N_TILES:
                 return
             if n % 2 == 0:
-                o_tiles[n // 2] = work.tile([P, 2, R], F32, name="o_tile")
+                o_tiles[n // 2] = work.tile([P, 2, R], F32, name="o_tile", bufs=8)
             nc.scalar.copy(out=o_tiles[n // 2][:, n % 2, :], in_=o_banks[n][:])
 
-        def store(m):
+        def store(m, j0, j1):
             h, js = where(m)
-            nc.sync.dma_start(out=o_view[h, :, js, :], in_=o_tiles[m][:])
+            nc.sync.dma_start(out=o_view[h, :, js.start + j0 : js.start + j1, :], in_=o_tiles[m][:, j0:j1, :])
 
         make_identity(nc, ident[:])
         nc.vector.memset(warm[:], 0.0)
@@ -243,27 +260,30 @@ def tile_anomaly_association_discrepancy_s14_kernel(
                 load_pair(m)
 
             turn_query(0)
-            turn_query(1)
-            for m in range(2):
-                copy_query(m, 0, nc.vector.tensor_copy)
-                copy_query(m, 1, nc.scalar.copy)
-                if m == 0:
-                    quantise_query(m)
+            for j in range(2):
+                copy_query(0, j, nc.scalar.copy if j else nc.vector.tensor_copy)
+                quantise_query(0, j, j + 1)
             multiply_keys(0)
             multiply_keys(1)
+            turn_query(1)
+            copy_query(1, 0, nc.scalar.copy)
+            copy_query(1, 1, nc.scalar.copy)
 
             for n in range(N_TILES + 3):
                 add_energy(n)
                 copy_disc(n - 2)
                 square(n)
                 times_prior(n - 1, 0, nc.vector)
-                times_prior(n, 1, nc.gpsimd)
+                if n == N_TILES:
+                    times_prior(n - 1, 1, nc.vector)
+                elif n < N_TILES - 1:
+                    times_prior(n, 1, nc.gpsimd)
                 quantise_disc(n - 2)
                 if n % 2:
                     copy_query((n + 3) // 2, 0, nc.vector.tensor_copy)
                     copy_query((n + 3) // 2, 1, nc.scalar.copy)
                 else:
-                    quantise_query((n + 2) // 2)
+                    quantise_query((n + 2) // 2, 0, 2)
                 copy_out(n - 3)
                 turn_disc(n - 1)
                 if n % 2 == 0:
@@ -272,5 +292,7 @@ def tile_anomaly_association_discrepancy_s14_kernel(
                 multiply_readout(n - 2)
                 if n % 2:
                     load_pair((n - 1) // 2 + LOOKAHEAD)
-                elif n >= 4:
-                    store((n - 4) // 2)
+                elif n >= 4 and n < N_TILES + 2:
+                    store((n - 4) // 2, 0, 2)
+                if n >= N_TILES + 1:
+                    store(N_PAIRS - 1, n - N_TILES - 1, n - N_TILES)

@@ -22,6 +22,7 @@ TILES = T // P
 N_TILES = H * TILES
 N_PAIRS = N_TILES // 2
 LOOKAHEAD = 5
+GP = 256
 
 
 def tile_anomaly_association_discrepancy_s14_kernel(
@@ -36,7 +37,7 @@ def tile_anomaly_association_discrepancy_s14_kernel(
     with ExitStack() as ctx:
         keep = ctx.enter_context(tc.tile_pool(name="keep", bufs=1))
         load = ctx.enter_context(tc.tile_pool(name="load", bufs=LOOKAHEAD + 1))
-        work = ctx.enter_context(tc.tile_pool(name="work", bufs=3))
+        work = ctx.enter_context(tc.tile_pool(name="work", bufs=4))
         score_pool = ctx.enter_context(tc.psum_pool(name="score_pool", bufs=4))
         turn_pool = ctx.enter_context(tc.psum_pool(name="turn_pool", bufs=2))
         out_pool = ctx.enter_context(tc.psum_pool(name="out_pool", bufs=2))
@@ -115,11 +116,12 @@ def tile_anomaly_association_discrepancy_s14_kernel(
             q_codes[m] = work.tile([P, 2 * P], U32, align_bytes=64, name="q_code")
             q_planes[m] = work.tile([P, 2 * P], U8, align_bytes=64, name="q_plane")
 
-        def copy_query(m, j, copy):
+        def copy_query(m, j0, j1, copy):
             if m >= N_PAIRS:
                 return
             dst = q_groups[m][:].bitcast(F32).rearrange("p (j r u) -> p j r u", j=2, u=2)
-            copy(out=dst[:, j], in_=q_banks[m][:, j].rearrange("p u r -> p r u"))
+            src = q_banks[m][:].rearrange("p j u r -> p j r u")
+            copy(out=dst[:, j0:j1], in_=src[:, j0:j1])
 
         def quantise_query(m, j0, j1):
             if m >= N_PAIRS:
@@ -169,15 +171,11 @@ def tile_anomaly_association_discrepancy_s14_kernel(
                 nc.scalar.activation(out=squares[n][:, c : c + width], in_=ratios[n][:, c : c + width], func=SQUARE)
             discs[n] = work.tile([P, L], BF16, align_bytes=64, name="disc")
 
-        def times_prior(n, half, engine):
+        def times_prior(n, c0, c1, engine):
             if not 0 <= n < N_TILES:
                 return
-            cols = slice(512 * half, 512 * half + 512)
             engine.tensor_tensor(
-                out=discs[n][:, cols].rearrange("p (u w e) -> p u w e", u=2, e=2),
-                in0=squares[n][:, cols].rearrange("p (w u e) -> p u w e", u=2, e=2),
-                in1=p_tiles[n // 2][:, n % 2, cols].rearrange("p (w u e) -> p u w e", u=2, e=2),
-                op=MULT,
+                out=discs[n][:, c0:c1], in0=squares[n][:, c0:c1], in1=p_tiles[n // 2][:, n % 2, c0:c1], op=MULT
             )
 
         def turn_disc(n):
@@ -185,8 +183,11 @@ def tile_anomaly_association_discrepancy_s14_kernel(
                 return
             bank = turn_pool.tile([P, 2, 2, P], F32, name="turn")
             words = discs[n][:].bitcast(F32)
-            for s in range(4):
-                nc.tensor.transpose(bank[:, s // 2, s % 2, :], words[:, P * s : P * s + P], ident[:])
+            for g in range(2):
+                for u in range(2):
+                    nc.tensor.transpose(
+                        bank[:, g, u, :], words[:, 2 * P * g + u : 2 * P * (g + 1) : 2], ident[:]
+                    )
             d_banks[n] = bank
 
         def copy_disc(n):
@@ -261,38 +262,38 @@ def tile_anomaly_association_discrepancy_s14_kernel(
 
             turn_query(0)
             for j in range(2):
-                copy_query(0, j, nc.scalar.copy if j else nc.vector.tensor_copy)
+                copy_query(0, j, j + 1, nc.scalar.copy if j else nc.vector.tensor_copy)
                 quantise_query(0, j, j + 1)
             multiply_keys(0)
             multiply_keys(1)
             turn_query(1)
-            copy_query(1, 0, nc.scalar.copy)
-            copy_query(1, 1, nc.scalar.copy)
+            copy_query(1, 0, 2, nc.scalar.copy)
 
-            for n in range(N_TILES + 3):
+            for n in range(N_TILES + 5):
                 add_energy(n)
-                copy_disc(n - 2)
+                copy_disc(n - 3)
                 square(n)
-                times_prior(n - 1, 0, nc.vector)
                 if n == N_TILES:
-                    times_prior(n - 1, 1, nc.vector)
-                elif n < N_TILES - 1:
-                    times_prior(n, 1, nc.gpsimd)
-                quantise_disc(n - 2)
+                    times_prior(n - 1, 0, L // 2, nc.vector)
+                    times_prior(n - 1, L // 2, L, nc.vector)
+                else:
+                    times_prior(n - 1, 0, L - GP, nc.vector)
+                    if n < N_TILES - 1:
+                        times_prior(n, L - GP, L, nc.gpsimd)
+                quantise_disc(n - 3)
                 if n % 2:
-                    copy_query((n + 3) // 2, 0, nc.vector.tensor_copy)
-                    copy_query((n + 3) // 2, 1, nc.scalar.copy)
+                    copy_query((n + 3) // 2, 0, 2, nc.scalar.copy)
                 else:
                     quantise_query((n + 2) // 2, 0, 2)
-                copy_out(n - 3)
-                turn_disc(n - 1)
+                copy_out(n - 5)
+                turn_disc(n - 2)
                 if n % 2 == 0:
                     turn_query((n + 4) // 2)
                 multiply_keys(n + 2)
-                multiply_readout(n - 2)
+                multiply_readout(n - 4)
                 if n % 2:
                     load_pair((n - 1) // 2 + LOOKAHEAD)
-                elif n >= 4 and n < N_TILES + 2:
-                    store((n - 4) // 2, 0, 2)
-                if n >= N_TILES + 1:
-                    store(N_PAIRS - 1, n - N_TILES - 1, n - N_TILES)
+                elif n >= 6 and n < N_TILES + 4:
+                    store((n - 6) // 2, 0, 2)
+                if n >= N_TILES + 3:
+                    store(N_PAIRS - 1, n - N_TILES - 3, n - N_TILES - 2)

@@ -22,7 +22,8 @@ TILES = T // P
 N_TILES = H * TILES
 N_PAIRS = N_TILES // 2
 LOOKAHEAD = 5
-GP = 256
+VECTOR_COPIES = (26, 28, 30)
+GP = 288
 
 
 def tile_anomaly_association_discrepancy_s14_kernel(
@@ -235,7 +236,8 @@ def tile_anomaly_association_discrepancy_s14_kernel(
                 return
             if n % 2 == 0:
                 o_tiles[n // 2] = work.tile([P, 2, R], F32, name="o_tile", bufs=8)
-            nc.scalar.copy(out=o_tiles[n // 2][:, n % 2, :], in_=o_banks[n][:])
+            copy = nc.vector.tensor_copy if n in VECTOR_COPIES else nc.scalar.copy
+            copy(out=o_tiles[n // 2][:, n % 2, :], in_=o_banks[n][:])
 
         def store(m, j0, j1):
             h, js = where(m)
@@ -250,9 +252,9 @@ def tile_anomaly_association_discrepancy_s14_kernel(
             nc.scalar.activation(out=warm[:], in_=warm[:], func=SQUARE)
             load_query(0)
             load_scales(k_scales, key_scales)
+            load_query(1)
             load_keys(0)
             load_energy(0)
-            load_query(1)
             load_prior(0)
             load_query(2)
             load_scales(r_scales, read_scales)
@@ -261,18 +263,20 @@ def tile_anomaly_association_discrepancy_s14_kernel(
                 load_pair(m)
 
             turn_query(0)
+            turn_query(1)
             for j in range(2):
                 copy_query(0, j, j + 1, nc.scalar.copy if j else nc.vector.tensor_copy)
                 quantise_query(0, j, j + 1)
             multiply_keys(0)
             multiply_keys(1)
-            turn_query(1)
             copy_query(1, 0, 2, nc.scalar.copy)
 
             for n in range(N_TILES + 5):
                 add_energy(n)
                 copy_disc(n - 3)
                 square(n)
+                if n % 2 == 0:
+                    quantise_query((n + 2) // 2, 0, 2)
                 if n == N_TILES:
                     times_prior(n - 1, 0, L // 2, nc.vector)
                     times_prior(n - 1, L // 2, L, nc.vector)
@@ -283,8 +287,6 @@ def tile_anomaly_association_discrepancy_s14_kernel(
                 quantise_disc(n - 3)
                 if n % 2:
                     copy_query((n + 3) // 2, 0, 2, nc.scalar.copy)
-                else:
-                    quantise_query((n + 2) // 2, 0, 2)
                 copy_out(n - 5)
                 turn_disc(n - 2)
                 if n % 2 == 0:

from contextlib import ExitStack

import concourse.mybir as mybir
from concourse.masks import make_identity

H, T, D, L, R = 4, 1024, 512, 1024, 512
FLOPS = 2 * H * T * D * L + 2 * H * T * L * R

F32 = mybir.dt.float32
BF16 = mybir.dt.bfloat16
I32 = mybir.dt.int32
U32 = mybir.dt.uint32
U8 = mybir.dt.uint8
FP8X4 = mybir.dt.float8_e4m3fn_x4
FP4X4 = mybir.dt.float4_e2m1fn_x4
MULT = mybir.AluOpType.mult
ADD = mybir.AluOpType.add
SQUARE = mybir.ActivationFunctionType.Square

P = 128
TILES = T // P
N_TILES = H * TILES
N_PAIRS = N_TILES // 2
LOOKAHEAD = 5
VECTOR_COPIES = (26, 28, 30)
GP = 288


def tile_anomaly_association_discrepancy_s14_kernel(
    tc, query, energy, prior, key_words, key_scales, read_words, read_scales, out
):
    nc = tc.nc
    q_view = query.rearrange("h (p j) d -> h p j d", j=TILES)
    e_view = energy.rearrange("h (p j) l -> h p j l", j=TILES)
    p_view = prior.rearrange("h (p j) l -> h p j l", j=TILES)
    o_view = out.rearrange("h (p j) r -> h p j r", j=TILES)

    with ExitStack() as ctx:
        keep = ctx.enter_context(tc.tile_pool(name="keep", bufs=1))
        load = ctx.enter_context(tc.tile_pool(name="load", bufs=LOOKAHEAD + 1))
        work = ctx.enter_context(tc.tile_pool(name="work", bufs=4))
        score_pool = ctx.enter_context(tc.psum_pool(name="score_pool", bufs=4))
        turn_pool = ctx.enter_context(tc.psum_pool(name="turn_pool", bufs=2))
        out_pool = ctx.enter_context(tc.psum_pool(name="out_pool", bufs=2))

        ident = keep.tile([P, P], F32)
        warm = keep.tile([P, 1], F32)
        k_words = [keep.tile([P, 2 * L], U8, align_bytes=64, name="k_words%d" % h) for h in range(H)]
        r_words = [keep.tile([P, 2, 2 * R], U8, align_bytes=64, name="r_words%d" % h) for h in range(H)]
        k_scales = keep.tile([P, H, L], U8, align_bytes=64)
        r_scales = keep.tile([P, 2 * H, R], U8, align_bytes=64)

        q_tiles, e_tiles, p_tiles = {}, {}, {}
        q_codes, q_planes, q_banks, q_groups = {}, {}, {}, {}
        scores, ratios, squares, discs = {}, {}, {}, {}
        d_banks, d_groups, d_codes, d_planes = {}, {}, {}, {}
        o_banks, o_tiles = {}, {}

        def where(m):
            return m // (TILES // 2), slice(2 * (m % (TILES // 2)), 2 * (m % (TILES // 2)) + 2)

        def parts(n):
            return 2 if n == N_TILES - 1 else 1

        def load_query(m):
            if m >= N_PAIRS:
                return
            h, js = where(m)
            q_tiles[m] = load.tile([P, 2, D], BF16, name="q_tile")
            nc.sync.dma_start(out=q_tiles[m][:], in_=q_view[h, :, js, :])

        def load_energy(m):
            h, js = where(m)
            e_tiles[m] = load.tile([P, 2, L], BF16, name="e_tile")
            nc.sync.dma_start(out=e_tiles[m][:], in_=e_view[h, :, js, :])

        def load_prior(m):
            h, js = where(m)
            p_tiles[m] = load.tile([P, 2, L], BF16, name="p_tile")
            nc.sync.dma_start(out=p_tiles[m][:], in_=p_view[h, :, js, :])

        def load_keys(h):
            nc.sync.dma_start(out=k_words[h][:].bitcast(I32), in_=key_words[h].bitcast(I32))

        def load_readout(h):
            nc.sync.dma_start(
                out=r_words[h][:].bitcast(I32),
                in_=read_words[2 * h : 2 * h + 2].bitcast(I32).rearrange("g p n -> p g n"),
            )

        def load_scales(plane, scales):
            rows = scales.bitcast(I32).rearrange("g (q r) n -> r q g n", r=4)
            for r in range(4):
                nc.sync.dma_start(out=plane[r:P:32, :, :].bitcast(I32), in_=rows[r])

        def load_pair(m):
            if m >= N_PAIRS:
                return
            load_energy(m)
            load_prior(m)
            load_query(m + 2)
            h, rest = divmod(m + 3, TILES // 2)
            if rest == 0 and h < H:
                load_keys(h)
                load_readout(h)

        def turn_query(m):
            if m >= N_PAIRS:
                return
            bank = turn_pool.tile([P, 2, 2, P], F32, name="turn")
            for j in range(2):
                words = q_tiles[m][:, j, :].bitcast(F32)
                for u in range(2):
                    nc.tensor.transpose(bank[:, j, u, :], words[:, u : D // 2 : 2], ident[:])
            q_banks[m] = bank
            q_groups[m] = work.tile([P, 2 * P * 4], BF16, align_bytes=64, name="q_group", bufs=2)
            q_codes[m] = work.tile([P, 2 * P], U32, align_bytes=64, name="q_code")
            q_planes[m] = work.tile([P, 2 * P], U8, align_bytes=64, name="q_plane")

        def copy_query(m, j0, j1, copy):
            if m >= N_PAIRS:
                return
            dst = q_groups[m][:].bitcast(F32).rearrange("p (j r u) -> p j r u", j=2, u=2)
            src = q_banks[m][:].rearrange("p j u r -> p j r u")
            copy(out=dst[:, j0:j1], in_=src[:, j0:j1])

        def quantise_query(m, j0, j1):
            if m >= N_PAIRS:
                return
            cols = slice(P * j0, P * j1)
            nc.vector.quantize_mx(
                out=q_codes[m][:, cols].bitcast(FP8X4),
                scales=q_planes[m][:, cols],
                in_=q_groups[m][:, 4 * P * j0 : 4 * P * j1],
            )

        def multiply_keys(n):
            if n >= N_TILES:
                return
            m, h = n // 2, n // TILES
            cols = slice((n % 2) * P, (n % 2) * P + P)
            scores[n] = []
            for half in range(2):
                bank = score_pool.tile([P, 512], F32, name="score")
                nc.tensor.matmul_mx(
                    out=bank[:],
                    lhsT=q_codes[m][:, cols].bitcast(FP8X4),
                    lhsT_scale=q_planes[m][:, cols],
                    rhs=k_words[h][:, 1024 * half : 1024 * half + 1024].bitcast(FP4X4),
                    rhs_scale=k_scales[:, h, 512 * half : 512 * half + 512],
                    start=True,
                    stop=True,
                )
                scores[n].append(bank)

        def add_energy(n):
            if n >= N_TILES:
                return
            ratios[n] = work.tile([P, L], F32, name="ratio")
            for half in range(2):
                cols = slice(512 * half, 512 * half + 512)
                nc.vector.tensor_tensor(
                    out=ratios[n][:, cols], in0=scores[n][half][:], in1=e_tiles[n // 2][:, n % 2, cols], op=ADD
                )

        def square(n):
            if n >= N_TILES:
                return
            squares[n] = work.tile([P, L], F32, name="square_tile")
            width = L // parts(n)
            for c in range(0, L, width):
                nc.scalar.activation(out=squares[n][:, c : c + width], in_=ratios[n][:, c : c + width], func=SQUARE)
            discs[n] = work.tile([P, L], BF16, align_bytes=64, name="disc")

        def times_prior(n, c0, c1, engine):
            if not 0 <= n < N_TILES:
                return
            engine.tensor_tensor(
                out=discs[n][:, c0:c1], in0=squares[n][:, c0:c1], in1=p_tiles[n // 2][:, n % 2, c0:c1], op=MULT
            )

        def turn_disc(n):
            if not 0 <= n < N_TILES:
                return
            bank = turn_pool.tile([P, 2, 2, P], F32, name="turn")
            words = discs[n][:].bitcast(F32)
            for g in range(2):
                for u in range(2):
                    nc.tensor.transpose(
                        bank[:, g, u, :], words[:, 2 * P * g + u : 2 * P * (g + 1) : 2], ident[:]
                    )
            d_banks[n] = bank

        def copy_disc(n):
            if not 0 <= n < N_TILES:
                return
            d_groups[n] = work.tile([P, L], BF16, align_bytes=64, name="d_group")
            dst = d_groups[n][:].bitcast(F32).rearrange("p (g r u) -> p g r u", g=2, u=2)
            src = d_banks[n][:].rearrange("p g u r -> p g r u")
            width = 2 // parts(n)
            for g in range(0, 2, width):
                nc.scalar.copy(out=dst[:, g : g + width], in_=src[:, g : g + width])

        def quantise_disc(n):
            if not 0 <= n < N_TILES:
                return
            d_codes[n] = work.tile([P, 2 * P], U32, align_bytes=64, name="d_code")
            d_planes[n] = work.tile([P, 2 * P], U8, align_bytes=64, name="d_plane")
            width = 2 * P // parts(n)
            for c in range(0, 2 * P, width):
                nc.vector.quantize_mx(
                    out=d_codes[n][:, c : c + width].bitcast(FP8X4),
                    scales=d_planes[n][:, c : c + width],
                    in_=d_groups[n][:, 4 * c : 4 * (c + width)],
                )

        def multiply_readout(n):
            if not 0 <= n < N_TILES:
                return
            h = n // TILES
            o_banks[n] = out_pool.tile([P, R], F32, name="o_bank")
            for g in range(2):
                cols = slice(P * g, P * g + P)
                nc.tensor.matmul_mx(
                    out=o_banks[n][:],
                    lhsT=d_codes[n][:, cols].bitcast(FP8X4),
                    lhsT_scale=d_planes[n][:, cols],
                    rhs=r_words[h][:, g, :].bitcast(FP4X4),
                    rhs_scale=r_scales[:, 2 * h + g, :],
                    start=(g == 0),
                    stop=(g == 1),
                )

        def copy_out(n):
            if not 0 <= n < N_TILES:
                return
            if n % 2 == 0:
                o_tiles[n // 2] = work.tile([P, 2, R], F32, name="o_tile", bufs=8)
            copy = nc.vector.tensor_copy if n in VECTOR_COPIES else nc.scalar.copy
            copy(out=o_tiles[n // 2][:, n % 2, :], in_=o_banks[n][:])

        def store(m, j0, j1):
            h, js = where(m)
            nc.sync.dma_start(out=o_view[h, :, js.start + j0 : js.start + j1, :], in_=o_tiles[m][:, j0:j1, :])

        make_identity(nc, ident[:])
        nc.vector.memset(warm[:], 0.0)
        nc.vector.memset(k_scales[:].bitcast(I32), 0)
        nc.vector.memset(r_scales[:].bitcast(I32), 0)

        with tc.manual_schedule():
            nc.scalar.activation(out=warm[:], in_=warm[:], func=SQUARE)
            load_query(0)
            load_scales(k_scales, key_scales)
            load_query(1)
            load_keys(0)
            load_energy(0)
            load_prior(0)
            load_query(2)
            load_scales(r_scales, read_scales)
            load_readout(0)
            for m in range(1, LOOKAHEAD):
                load_pair(m)

            turn_query(0)
            turn_query(1)
            for j in range(2):
                copy_query(0, j, j + 1, nc.scalar.copy if j else nc.vector.tensor_copy)
                quantise_query(0, j, j + 1)
            multiply_keys(0)
            multiply_keys(1)
            copy_query(1, 0, 2, nc.scalar.copy)

            for n in range(N_TILES + 5):
                add_energy(n)
                copy_disc(n - 3)
                square(n)
                if n % 2 == 0:
                    quantise_query((n + 2) // 2, 0, 2)
                if n == N_TILES:
                    times_prior(n - 1, 0, L // 2, nc.vector)
                    times_prior(n - 1, L // 2, L, nc.vector)
                else:
                    times_prior(n - 1, 0, L - GP, nc.vector)
                    if n < N_TILES - 1:
                        times_prior(n, L - GP, L, nc.gpsimd)
                quantise_disc(n - 3)
                if n % 2:
                    copy_query((n + 3) // 2, 0, 2, nc.scalar.copy)
                copy_out(n - 5)
                turn_disc(n - 2)
                if n % 2 == 0:
                    turn_query((n + 4) // 2)
                multiply_keys(n + 2)
                multiply_readout(n - 4)
                if n % 2:
                    load_pair((n - 1) // 2 + LOOKAHEAD)
                elif n >= 6 and n < N_TILES + 4:
                    store((n - 6) // 2, 0, 2)
                if n >= N_TILES + 3:
                    store(N_PAIRS - 1, n - N_TILES - 3, n - N_TILES - 2)
